import numpy as np, ml_dtypes
CORES = [9,10,11,14,17,18,19,22,49,50,51,54]
N = 12
import mx_ref
NC, G = 256, 4
C, C2 = np.float32(0.023), np.float32(0.029)
CNT = [[24,8,0,16,8,120,32,0,24,24,0,0],[24,8,0,0,8,8,40,56,64,0,24,24],[24,72,0,0,0,0,32,24,8,32,64,0],[32,0,24,32,104,0,24,8,0,8,24,0],[0,32,24,88,32,0,24,16,32,0,8,0],[8,32,64,8,8,48,0,0,32,8,0,48],[16,24,0,24,8,48,0,96,8,8,8,16],[64,0,0,32,16,8,16,24,32,24,32,8],[48,0,48,24,0,0,8,0,0,56,8,64],[8,16,8,0,72,16,72,0,0,8,0,56],[8,24,56,32,0,8,0,0,0,24,64,40],[0,40,32,0,0,0,8,32,56,64,24,0]]
OFF = [[sum(c[:e]) for e in range(N + 1)] for c in CNT]
BF = ml_dtypes.bfloat16
def cut(t, i, w=512):
    return t[:, w * i:w * i + w]
def tile(rs):
    return np.stack(rs, axis=2).reshape(128, -1).astype(BF)
def layer(w, X):
    out = []
    for i in range(G):
        for t in range(len(X)):
            p = mx_ref.matmul(mx_ref.quantize(cut(w, len(X) * i + t)), X[t])
            z = p if t == 0 else z + p
        out.append(z)
    return out
def act(Z):
    return [np.maximum(z, 0) * C for z in Z]
def setup_inputs(rng):
    def f(*shape):
        return mx_ref.flush((rng.standard_normal(shape, dtype=np.float32) * np.exp2(rng.integers(-2, 3, shape[:-1] + (1,)))).astype(BF))
    return {"x": f(N, 128, 4 * NC), "w1": f(N, 128, G * 512), "w2": f(N, 128, G * 512), "w3": f(N, 128, 512)}
def setup_inputs_blocks(rng):
    d = setup_inputs(rng)
    for k in ("x", "w3"): d[k] = mx_ref.spread(d[k], rng, 4)
    for k in ("w1", "w2"): d[k] = mx_ref.spread(d[k], rng, 2)
    return d
def setup_inputs_wide(rng):
    d = setup_inputs(rng)
    for k in ("x", "w1", "w2", "w3"): d[k] = mx_ref.flush((d[k].astype(np.float32) * np.exp2(rng.integers(-4, 5, (N, 1, 1))).astype(np.float32)).astype(BF))
    return d
def setup_inputs_zeros(rng):
    d = setup_inputs(rng); v = d["x"].reshape(N, 128, -1, 4).copy()
    v[np.broadcast_to((rng.random((N, 1, v.shape[2], 1)) < 0.33), v.shape)] = 0
    d["x"] = v.reshape(d["x"].shape)
    return d
def act2(Z):
    return [np.maximum(z, 0) * C2 for z in Z]
def reference(x, w1, w2, w3):
    h = [tile(act(layer(w1[j], [mx_ref.quantize(x[j])]))) for j in range(N)]
    g = []
    for e in range(N):
        t = np.concatenate([h[j][:, 4 * OFF[j][e]:4 * OFF[j][e + 1]] for j in range(N)], axis=1)
        g.append(tile(act2(layer(w2[e], [mx_ref.quantize(t)]))))
    y = np.zeros((N, 128, NC), np.float32)
    for j in range(N):
        back = []
        for e in range(N):
            a = sum(CNT[i][e] for i in range(j))
            back.append(g[e][:, 4 * a:4 * a + 4 * CNT[j][e]])
        y[j] = mx_ref.matmul(mx_ref.quantize(w3[j]), mx_ref.quantize(np.concatenate(back, axis=1)))
    return {"y": y}

@@ -1,0 +1,277 @@
+from concourse.bass import DstId, RemoteDMATransfer
+from concourse.mybir import dt, AluOpType, ActivationFunctionType
+
+SIM_CORES = 64
+NC = 256
+W = 128
+G = 4
+C1, C2 = 0.023, 0.029
+
+CODES, BYTES = "float8_e4m3fn_x4", "uint8"
+SCRATCH = {
+    "xs": ("sbuf", [128, 4 * NC], "bfloat16"),
+    "w1s": ("sbuf", [128, 4 * G * W], "bfloat16"),
+    "w2s": ("sbuf", [128, 4 * G * W], "bfloat16"),
+    "w3s": ("sbuf", [128, 4 * W], "bfloat16"),
+    "ht": ("sbuf", [128, 4 * NC], "bfloat16"),
+    "gt": ("sbuf", [128, 4 * NC], "bfloat16"),
+    "ys": ("sbuf", [128, NC], "float32"),
+    "xq": ("sbuf", [128, NC], CODES), "xp": ("sbuf", [128, NC], BYTES),
+    "w1q": ("sbuf", [128, G * W], CODES), "w1p": ("sbuf", [128, G * W], BYTES),
+    "w2q": ("sbuf", [128, G * W], CODES), "w2p": ("sbuf", [128, G * W], BYTES),
+    "w3q": ("sbuf", [128, W], CODES), "w3p": ("sbuf", [128, W], BYTES),
+    "cb": ("sbuf", [128, 2 * NC], CODES), "cp": ("sbuf", [128, 2 * NC], BYTES),
+    "gb": ("sbuf", [128, 2 * NC], CODES), "gp": ("sbuf", [128, 2 * NC], BYTES),
+    "rq0": ("sbuf", [128, NC], CODES), "rp0": ("sbuf", [128, NC], BYTES),
+    "rq1": ("sbuf", [128, NC], CODES), "rp1": ("sbuf", [128, NC], BYTES),
+    "ps": ("psum", [128, 4096], "float32"),
+}
+SEMAPHORES = ["xl", "w1a", "w1b", "w2l", "w3l", "qx", "qa", "qb", "q2", "q3", "hq", "gq",
+              "z0", "z1", "z2", "z3", "y0", "y1", "y2", "y3", "f0", "f1",
+              "ahs", "ahv", "ags", "agv", "ysv", "yss", "st",
+              "arr0", "arr1", "rel0", "rel1", "loc"]
+
+
+def bits(m):
+    return [k for k in range(16) if m >> k & 1]
+
+
+def widths(ph, a, b, cnt):
+    return cnt[a][b] if ph == 0 else cnt[b][a]
+
+
+def places(cnt, n):
+    hpos = [[0] * n for _ in range(n)]
+    gpos = [[0] * n for _ in range(n)]
+    for j in range(n):
+        a = b = 0
+        for k in range(n):
+            e = (j + 1 + k) % n
+            hpos[j][e] = a
+            a += cnt[j][e]
+            s = (j + k) % n
+            gpos[j][s] = b
+            b += cnt[s][j]
+    return hpos, gpos
+
+
+def relays(cores, topo):
+    used, out = set(cores), {}
+    chips = sorted(set(topo.chip(c) for c in cores))
+    for j, s in enumerate(cores):
+        for ch in chips:
+            dst = [c for c in cores if topo.chip(c) == ch]
+            if all(c == s or topo.may_write(s, c) for c in dst):
+                continue
+            pick = []
+            for near in (True, False):
+                r = [c for c in range(SIM_CORES) if c not in used and topo.mates(topo.chip(c), ch)
+                     and (topo.die(c) == topo.die(s)) == near
+                     and topo.may_write(s, c) and all(topo.may_write(c, d) for d in dst)][0]
+                used.add(r)
+                pick.append(r)
+            out[(j, ch)] = pick
+    return out
+
+
+def deal(items, src, load, topo):
+    away = [c for c in range(SIM_CORES) if topo.chip(c) != topo.chip(src)]
+    off = bits(topo.mask(src, away[0]))
+    res = []
+    for far in (True, False):
+        grp = [t for t in items if (topo.chip(t[0]) != topo.chip(src)) == far]
+        if not grp:
+            continue
+        pool = off if far else [k for k in bits(topo.mask(src, grp[0][0])) if k not in off]
+        size = [1] * len(grp)
+        while True:
+            k = min(range(len(grp)), key=lambda i: size[i])
+            if sum(size) + size[k] > len(pool):
+                break
+            size[k] *= 2
+        free = sorted(pool, key=lambda k: load[k])
+        for i in sorted(range(len(grp)), key=lambda i: size[i]):
+            eng, free = free[:size[i]], free[size[i]:]
+            for k in eng:
+                load[k] += 128 // size[i]
+            res.append((grp[i], eng))
+    return res
+
+
+def plan(T, topo):
+    cnt, cores = T.tables["CNT"], T.cores
+    n = len(cores)
+    hpos, gpos = places(cnt, n)
+    rel = relays(cores, topo)
+    calls = {c: [] for c in range(SIM_CORES)}
+    load = {c: [0] * 16 for c in range(SIM_CORES)}
+
+    def emit(c, wait, items):
+        groups = {}
+        for t in items:
+            groups.setdefault(t[6] * (4 if t[1] == "q" else 1), []).append(t)
+        cut = []
+        for b, g in groups.items():
+            for i in range(0, len(g), 8):
+                cut.append((b, g[i:i + 8]))
+
+        def rank(bg):
+            far = sum(topo.chip(t[0]) != topo.chip(c) for t in bg[1])
+            return (-min(far, 1), -far, -bg[0])
+        for b, g in sorted(cut, key=rank):
+            calls[c].append((wait, deal(g, c, load[c], topo)))
+
+    for ph in range(2):
+        buf = {"q": ("cb", "gb")[ph], "p": ("cp", "gp")[ph]}
+        arr, rbuf, rsem = "arr%d" % ph, {"q": "rq%d" % ph, "p": "rp%d" % ph}, "rel%d" % ph
+
+        def spot(a, b):
+            if ph == 0:
+                return hpos[a][b], NC + gpos[b][a] - cnt[b][b]
+            return NC + gpos[a][b], cnt[b][b] + hpos[b][a]
+        for a in range(n):
+            first, rest, done = [], [], set()
+            for (j, ch), pick in rel.items():
+                if j != a:
+                    continue
+                dst = [b for b in range(n) if topo.chip(cores[b]) == ch]
+                done.update(dst)
+                run = [b for b in dst if widths(ph, a, b, cnt)]
+                if not run:
+                    continue
+                lo = min(spot(a, b)[0] for b in run)
+                w = sum(widths(ph, a, b, cnt) for b in run)
+                for kind, r in zip("qp", pick):
+                    first.append((r, kind, buf[kind], lo, rbuf[kind], 0, w, rsem))
+                    emit(r, rsem, [(cores[b], kind, rbuf[kind], spot(a, b)[0] - lo, buf[kind], spot(a, b)[1],
+                                    widths(ph, a, b, cnt), arr) for b in run])
+            for b in range(n):
+                w = widths(ph, a, b, cnt)
+                if b == a or b in done or not w:
+                    continue
+                for kind in "qp":
+                    rest.append((cores[b], kind, buf[kind], spot(a, b)[0], buf[kind], spot(a, b)[1], w, arr))
+            wait = ("hq", "gq")[ph]
+            emit(cores[a], wait, first)
+            emit(cores[a], wait, rest)
+    need, own = {}, {}
+    for c in calls:
+        for wait, group in calls[c]:
+            for t, eng in group:
+                need[(t[0], t[7])] = need.get((t[0], t[7]), 0) + len(eng)
+                own[c] = own.get(c, 0) + len(eng)
+    return calls, need, own
+
+
+def remote(g, core, T, topo, calls, need, own):
+    waited = set()
+    for wait, group in calls[core]:
+        if wait not in waited:
+            waited.add(wait)
+            g.wait_ge(T.sem[wait], need.get((core, wait), 1))
+        tr = []
+        for (dst, kind, sb, sc, db, dc, w, sem), eng in group:
+            src, out = T[sb][:, sc:sc + w], T[db][:, dc:dc + w]
+            if kind == "q":
+                src, out = src.bitcast(dt.uint8), out.bitcast(dt.uint8)
+            rid, pid, _ = topo.addr(dst)
+            tr.append((rid, pid, src, out, sum(1 << k for k in eng), T.sem[sem]))
+        if len(tr) == 1:
+            rid, pid, src, out, m, s = tr[0]
+            g.remote_dma(out, src, s, T.sem.loc, pid, rid, m)
+        else:
+            g.remote_dma_fused([RemoteDMATransfer(dst_ids=[DstId(rid=rid, pnc=pid)], dma_engine_mask=m, remote_sem=s,
+                                                  src=src, dst=out) for rid, pid, src, out, m, s in tr],
+                               local_sem=T.sem.loc)
+    if core in own:
+        g.wait_ge(T.sem.loc, own[core])
+
+
+def rank_program(g, core, T, topo):
+    calls, need, own = plan(T, topo)
+    rank = T.rank_of(core)
+    if rank is None:
+        remote(g, core, T, topo, calls, need, own)
+        return
+    cnt, S = T.tables["CNT"], T.sem
+    mine = cnt[rank][rank]
+    cut = sum(cnt[rank][rank + 1:])
+    RELU, COPY = ActivationFunctionType.Relu, ActivationFunctionType.Copy
+
+    if cut:
+        g.sync.dma_start(T.xs[:, 0:4 * cut], T.x[:, 4 * (NC - cut):4 * NC]).then_inc(S.xl, 16)
+    (g.scalar if cut else g.sync).dma_start(T.xs[:, 4 * cut:4 * NC], T.x[:, 0:4 * (NC - cut)]).then_inc(S.xl, 16)
+    half = 2 * G * W
+    g.sync.dma_start(T.w1s[:, 0:half], T.w1[:, 0:half]).then_inc(S.w1a, 16)
+    g.scalar.dma_start(T.w1s[:, half:2 * half], T.w1[:, half:2 * half]).then_inc(S.w1b, 16)
+    g.sync.dma_start(T.w2s[:], T.w2[:]).then_inc(S.w2l, 16)
+    g.sync.dma_start(T.w3s[:], T.w3[:]).then_inc(S.w3l, 16)
+
+    t = g.tensor
+    t.wait_ge(S.qx, 1)
+    for i in range(G):
+        if i % 2 == 0:
+            t.wait_ge(S["qa" if i == 0 else "qb"], 1)
+        t.matmul_mx(T.ps[:, 512 * i:512 * i + NC], T.w1q[:, W * i:W * i + W], T.w1p[:, W * i:W * i + W],
+                    T.xq[:], T.xp[:], True, True).then_inc(S["z%d" % i], 1)
+    t.wait_ge(S.hq, 1)
+    t.wait_ge(S.q2, 1)
+    t.wait_ge(S.arr0, need[(core, "arr0")])
+    lo = NC - mine
+    for i in range(G):
+        t.matmul_mx(T.ps[:, 2048 + 512 * i:2048 + 512 * i + NC], T.w2q[:, W * i:W * i + W], T.w2p[:, W * i:W * i + W],
+                    T.cb[:, lo:lo + NC], T.cp[:, lo:lo + NC], True, True).then_inc(S["y%d" % i], 1)
+    t.wait_ge(S.gq, 1)
+    t.wait_ge(S.q3, 1)
+    t.wait_ge(S.arr1, need[(core, "arr1")])
+    for i in range(2):
+        a = mine + W * i
+        t.matmul_mx(T.ps[:, 512 * i:512 * i + W], T.w3q[:], T.w3p[:], T.gb[:, a:a + W], T.gp[:, a:a + W],
+                    True, True).then_inc(S["f%d" % i], 1)
+
+    sc = g.scalar
+    for base, tile, c, z, done in ((0, T.ht, C1, "z", S.ahs), (2048, T.gt, C2, "y", S.ags)):
+        for i in (0, 2):
+            sc.wait_ge(S[z + str(i)], 1)
+            sc.activation(tile[:, i:4 * NC:4], T.ps[:, base + 512 * i:base + 512 * i + NC], RELU,
+                          scale=c).then_inc(done, 1)
+
+    v = g.vector
+    v.wait_ge(S.xl, 32 if 0 < cut < NC else 16)
+    v.quantize_mx(T.xq[:], T.xp[:], T.xs[:]).then_inc(S.qx, 1)
+    for k, (ld, q) in enumerate(((S.w1a, S.qa), (S.w1b, S.qb))):
+        v.wait_ge(ld, 16)
+        v.quantize_mx(T.w1q[:, 2 * W * k:2 * W * k + 2 * W], T.w1p[:, 2 * W * k:2 * W * k + 2 * W],
+                      T.w1s[:, half * k:half * k + half]).then_inc(q, 1)
+
+    def acts(base, tile, c, z, ds, dv):
+        for i in (1, 3):
+            v.wait_ge(S[z + str(i)], 1)
+            v.tensor_scalar(tile[:, i:4 * NC:4], T.ps[:, base + 512 * i:base + 512 * i + NC], 0.0, c,
+                            AluOpType.max, AluOpType.mult).then_inc(dv, 1)
+        v.wait_ge(ds, 2)
+        v.wait_ge(dv, 2)
+    acts(0, T.ht, C1, "z", S.ahs, S.ahv)
+    v.quantize_mx(T.cb[:, 0:NC], T.cp[:, 0:NC], T.ht[:]).then_inc(S.hq, 1)
+    v.wait_ge(S.w2l, 16)
+    v.quantize_mx(T.w2q[:], T.w2p[:], T.w2s[:]).then_inc(S.q2, 1)
+    v.wait_ge(S.w3l, 16)
+    v.quantize_mx(T.w3q[:], T.w3p[:], T.w3s[:]).then_inc(S.q3, 1)
+    acts(2048, T.gt, C2, "y", S.ags, S.agv)
+    v.quantize_mx(T.gb[:, NC:2 * NC], T.gp[:, NC:2 * NC], T.gt[:]).then_inc(S.gq, 1)
+
+    for i, done in ((0, S.yss), (1, S.ysv)):
+        pieces = [(a, b) for a, b in ((W * i, min(W * i + W, cut)), (max(W * i, cut), W * i + W)) if a < b]
+        (sc if i == 0 else v).wait_ge(S["f%d" % i], 1)
+        for a, b in pieces:
+            k = (a - cut) % NC
+            src, out = T.ps[:, 512 * i + a - W * i:512 * i + b - W * i], T.ys[:, k:k + b - a]
+            if i == 0:
+                sc.activation(out, src, COPY).then_inc(done, 1)
+            else:
+                v.tensor_copy(out, src).then_inc(done, 1)
+        g.sync.wait_ge(done, len(pieces))
+    g.sync.dma_start(T.y[:], T.ys[:]).then_inc(S.st, 16)
+    g.sync.wait_ge(S.st, 16)
+
+    remote(g, core, T, topo, calls, need, own)

@@ -3,6 +3,7 @@ from concourse.mybir import dt, AluOpType, ActivationFunctionType
 
 SIM_CORES = 64
 NC = 256
+H = 128
 W = 128
 G = 4
 C1, C2 = 0.023, 0.029
@@ -26,33 +27,63 @@ SCRATCH = {
     "rq1": ("sbuf", [128, NC], CODES), "rp1": ("sbuf", [128, NC], BYTES),
     "ps": ("psum", [128, 4096], "float32"),
 }
-SEMAPHORES = ["xl", "w1a", "w1b", "w2l", "w3l", "qx", "qa", "qb", "q2", "q3", "hq", "gq",
-              "z0", "z1", "z2", "z3", "y0", "y1", "y2", "y3", "f0", "f1",
-              "ahs", "ahv", "ags", "agv", "ysv", "yss", "st",
-              "arr0", "arr1", "rel0", "rel1", "loc"]
+HALVES = (0, 1)
+SEMAPHORES = (["xl", "w1l0", "w1l1", "w1l2", "w2l", "w3l", "qx", "q1a0", "q1a1", "q1a2", "q2", "q3", "f0", "f1",
+               "ysv", "yss", "st", "loc", "arr00", "arr01", "arr1"]
+              + ["rel%d%d" % (p, h) for p in HALVES for h in HALVES]
+              + ["%s%d" % (s, h) for s in ("hq", "gq", "hs", "hv", "gs", "gv") for h in HALVES]
+              + ["%s%d%d" % (s, h, i) for s in "zy" for h in HALVES for i in range(G)])
+W1_CUTS = (0, 2, 3, 4)
 
 
 def bits(m):
     return [k for k in range(16) if m >> k & 1]
 
 
-def widths(ph, a, b, cnt):
-    return cnt[a][b] if ph == 0 else cnt[b][a]
+def may_chip(topo, src, cores, ch):
+    return all(c == src or topo.may_write(src, c) for c in cores if topo.chip(c) == ch)
 
 
-def places(cnt, n):
-    hpos = [[0] * n for _ in range(n)]
-    gpos = [[0] * n for _ in range(n)]
+def hit(items, target):
+    best = {0: []}
+    for name, size in items:
+        for s in sorted(best, reverse=True):
+            if s + size <= target and s + size not in best:
+                best[s + size] = best[s] + [name]
+    return best.get(target)
+
+
+def orders(T, topo):
+    cnt, cores = T.tables["CNT"], T.cores
+    n = len(cores)
+    ch = [topo.chip(c) for c in cores]
+    oh, og = [], []
     for j in range(n):
-        a = b = 0
-        for k in range(n):
-            e = (j + 1 + k) % n
-            hpos[j][e] = a
-            a += cnt[j][e]
-            s = (j + k) % n
-            gpos[j][s] = b
-            b += cnt[s][j]
-    return hpos, gpos
+        ring = [(j + 1 + k) % n for k in range(n)]
+        far = [e for e in sorted(ring) if not may_chip(topo, cores[j], cores, ch[e])]
+        oh.append(far + [e for e in ring if e not in far])
+    for e in range(n):
+        src = [j for j in range(n) if j != e and cnt[j][e]]
+        late = [j for j in src if not may_chip(topo, cores[j], cores, ch[e])]
+        near = [j for j in src if ch[j] == ch[e]]
+        rest = [j for j in src if j not in late and j not in near]
+        target = H - cnt[e][e]
+        early = None
+        if sum(cnt[j][e] for j in rest) >= target:
+            early = hit([(j, cnt[j][e]) for j in rest], target)
+        if early is None:
+            base = sum(cnt[j][e] for j in rest)
+            if base <= target:
+                more = hit([(j, cnt[j][e]) for j in near], target - base)
+                if more is not None:
+                    early = rest + more
+        if early is None:
+            early = hit([(j, cnt[j][e]) for j in rest + near], target)
+        if early is None:
+            early = rest
+        tail = sorted([j for j in src if j not in early], key=lambda j: (j in near, j))
+        og.append([e] + sorted(early) + tail + [j for j in range(n) if j != e and not cnt[j][e]])
+    return oh, og
 
 
 def relays(cores, topo):
@@ -61,7 +92,7 @@ def relays(cores, topo):
     for j, s in enumerate(cores):
         for ch in chips:
             dst = [c for c in cores if topo.chip(c) == ch]
-            if all(c == s or topo.may_write(s, c) for c in dst):
+            if may_chip(topo, s, cores, ch):
                 continue
             pick = []
             for near in (True, False):
@@ -101,59 +132,94 @@ def deal(items, src, load, topo):
 def plan(T, topo):
     cnt, cores = T.tables["CNT"], T.cores
     n = len(cores)
-    hpos, gpos = places(cnt, n)
+    oh, og = orders(T, topo)
+    hpos = [{e: sum(cnt[j][f] for f in oh[j][:oh[j].index(e)]) for e in range(n)} for j in range(n)]
+    gpos = [{j: sum(cnt[i][e] for i in og[e][:og[e].index(j)]) for j in range(n)} for e in range(n)]
     rel = relays(cores, topo)
     calls = {c: [] for c in range(SIM_CORES)}
     load = {c: [0] * 16 for c in range(SIM_CORES)}
 
-    def emit(c, wait, items):
+    def far(c, t):
+        return topo.chip(t[0]) != topo.chip(c)
+
+    def fuse(c, wait, items):
         groups = {}
         for t in items:
             groups.setdefault(t[6] * (4 if t[1] == "q" else 1), []).append(t)
-        cut = []
-        for b, g in groups.items():
-            for i in range(0, len(g), 8):
-                cut.append((b, g[i:i + 8]))
+        cut = [(b, g[i:i + 8]) for b, g in groups.items() for i in range(0, len(g), 8)]
 
         def rank(bg):
-            far = sum(topo.chip(t[0]) != topo.chip(c) for t in bg[1])
-            return (-min(far, 1), -far, -bg[0])
+            k = sum(far(c, t) for t in bg[1])
+            return (-min(k, 1), -k, -bg[0])
         for b, g in sorted(cut, key=rank):
             calls[c].append((wait, deal(g, c, load[c], topo)))
 
     for ph in range(2):
         buf = {"q": ("cb", "gb")[ph], "p": ("cp", "gp")[ph]}
-        arr, rbuf, rsem = "arr%d" % ph, {"q": "rq%d" % ph, "p": "rp%d" % ph}, "rel%d" % ph
+        rbuf = {"q": "rq%d" % ph, "p": "rp%d" % ph}
+
+        def cols(a, b):
+            return cnt[a][b] if ph == 0 else cnt[b][a]
 
         def spot(a, b):
             if ph == 0:
                 return hpos[a][b], NC + gpos[b][a] - cnt[b][b]
             return NC + gpos[a][b], cnt[b][b] + hpos[b][a]
+
+        def half(a, b):
+            return int(spot(a, b)[0] % NC + cols(a, b) > H)
+
+        def arr(a, b):
+            return "arr0%d" % int(gpos[b][a] >= H) if ph == 0 else "arr1"
         for a in range(n):
-            first, rest, done = [], [], set()
+            runs, direct, byrelay = {0: [], 1: []}, {0: [], 1: []}, set()
             for (j, ch), pick in rel.items():
                 if j != a:
                     continue
                 dst = [b for b in range(n) if topo.chip(cores[b]) == ch]
-                done.update(dst)
-                run = [b for b in dst if widths(ph, a, b, cnt)]
-                if not run:
-                    continue
-                lo = min(spot(a, b)[0] for b in run)
-                w = sum(widths(ph, a, b, cnt) for b in run)
-                for kind, r in zip("qp", pick):
-                    first.append((r, kind, buf[kind], lo, rbuf[kind], 0, w, rsem))
-                    emit(r, rsem, [(cores[b], kind, rbuf[kind], spot(a, b)[0] - lo, buf[kind], spot(a, b)[1],
-                                    widths(ph, a, b, cnt), arr) for b in run])
+                byrelay.update(dst)
+                at = 0
+                for hf in HALVES:
+                    run = sorted((spot(a, b)[0], b) for b in dst if cols(a, b) and half(a, b) == hf)
+                    part = []
+                    for p, b in run:
+                        if part and part[-1][0] + part[-1][1] == p:
+                            part[-1][1] += cols(a, b)
+                            part[-1][2].append(b)
+                        else:
+                            part.append([p, cols(a, b), [b]])
+                    for kind, r in zip("qp", pick):
+                        out, put = [], at
+                        for p, w, bs in part:
+                            runs[hf].append((r, kind, buf[kind], p, rbuf[kind], put, w, "rel%d%d" % (ph, hf)))
+                            out += [(cores[b], kind, rbuf[kind], put + spot(a, b)[0] - p, buf[kind], spot(a, b)[1],
+                                     cols(a, b), arr(a, b)) for b in bs]
+                            put += w
+                        fuse(r, "rel%d%d" % (ph, hf), out)
+                    at += sum(w for p, w, bs in part)
             for b in range(n):
-                w = widths(ph, a, b, cnt)
-                if b == a or b in done or not w:
+                if b == a or b in byrelay or not cols(a, b):
                     continue
                 for kind in "qp":
-                    rest.append((cores[b], kind, buf[kind], spot(a, b)[0], buf[kind], spot(a, b)[1], w, arr))
-            wait = ("hq", "gq")[ph]
-            emit(cores[a], wait, first)
-            emit(cores[a], wait, rest)
+                    direct[half(a, b)].append((cores[b], kind, buf[kind], spot(a, b)[0], buf[kind], spot(a, b)[1],
+                                               cols(a, b), arr(a, b)))
+            c, wait = cores[a], ["hq0", "hq1"] if ph == 0 else ["gq0", "gq1"]
+            if ph == 0:
+                soon = [t for t in direct[0] if far(c, t) and t[7] == "arr00"]
+                size = set(t[6] * (4 if t[1] == "q" else 1) for t in soon)
+                first = [t for t in direct[0] if t[6] * (4 if t[1] == "q" else 1) in size]
+                rest = [t for t in direct[0] if t not in first] + direct[1]
+                fuse(c, wait[0], runs[0])
+                fuse(c, wait[0], first)
+                fuse(c, wait[1], runs[1])
+                soon = [t for t in rest if far(c, t) and t[7] == "arr00"]
+                size = set(t[6] * (4 if t[1] == "q" else 1) for t in soon)
+                fuse(c, wait[1], [t for t in rest if t[6] * (4 if t[1] == "q" else 1) in size])
+                fuse(c, wait[1], [t for t in rest if t[6] * (4 if t[1] == "q" else 1) not in size])
+            else:
+                for hf in HALVES:
+                    fuse(c, wait[hf], runs[hf])
+                    fuse(c, wait[hf], direct[hf])
     need, own = {}, {}
     for c in calls:
         for wait, group in calls[c]:
@@ -195,82 +261,105 @@ def rank_program(g, core, T, topo):
         return
     cnt, S = T.tables["CNT"], T.sem
     mine = cnt[rank][rank]
-    cut = sum(cnt[rank][rank + 1:])
     RELU, COPY = ActivationFunctionType.Relu, ActivationFunctionType.Copy
+    t, sc, v = g.tensor, g.scalar, g.vector
 
-    if cut:
-        g.sync.dma_start(T.xs[:, 0:4 * cut], T.x[:, 4 * (NC - cut):4 * NC]).then_inc(S.xl, 16)
-    (g.scalar if cut else g.sync).dma_start(T.xs[:, 4 * cut:4 * NC], T.x[:, 0:4 * (NC - cut)]).then_inc(S.xl, 16)
-    half = 2 * G * W
-    g.sync.dma_start(T.w1s[:, 0:half], T.w1[:, 0:half]).then_inc(S.w1a, 16)
-    g.scalar.dma_start(T.w1s[:, half:2 * half], T.w1[:, half:2 * half]).then_inc(S.w1b, 16)
+    piece, at = [], 0
+    for e in orders(T, topo)[0][rank]:
+        o, w = sum(cnt[rank][:e]), cnt[rank][e]
+        if w and piece and piece[-1][1] + piece[-1][2] == o:
+            piece[-1][2] += w
+        elif w:
+            piece.append([at, o, w])
+        at += w
+
+    for k, (p, o, w) in enumerate(piece):
+        (g.sync if k % 2 == 0 else sc).dma_start(T.xs[:, 4 * p:4 * p + 4 * w], T.x[:, 4 * o:4 * o + 4 * w]).then_inc(S.xl, 16)
+    for k, q in enumerate((g.sync, sc, g.sync)):
+        a, b = 4 * W * W1_CUTS[k], 4 * W * W1_CUTS[k + 1]
+        q.dma_start(T.w1s[:, a:b], T.w1[:, a:b]).then_inc(S["w1l%d" % k], 16)
     g.sync.dma_start(T.w2s[:], T.w2[:]).then_inc(S.w2l, 16)
     g.sync.dma_start(T.w3s[:], T.w3[:]).then_inc(S.w3l, 16)
 
-    t = g.tensor
+    def bank(h, i):
+        return T.ps[:, 2048 * h + 512 * i:2048 * h + 512 * i + H]
+
+    def product(h, i, w, wp, m, mp, lo, sem):
+        t.matmul_mx(bank(h, i), w[:, W * i:W * i + W], wp[:, W * i:W * i + W], m[:, lo + H * h:lo + H * h + H],
+                    mp[:, lo + H * h:lo + H * h + H], True, True).then_inc(S["%s%d%d" % (sem, h, i)], 1)
     t.wait_ge(S.qx, 1)
-    for i in range(G):
-        if i % 2 == 0:
-            t.wait_ge(S["qa" if i == 0 else "qb"], 1)
-        t.matmul_mx(T.ps[:, 512 * i:512 * i + NC], T.w1q[:, W * i:W * i + W], T.w1p[:, W * i:W * i + W],
-                    T.xq[:], T.xp[:], True, True).then_inc(S["z%d" % i], 1)
-    t.wait_ge(S.hq, 1)
+    for k in range(3):
+        t.wait_ge(S["q1a%d" % k], 1)
+        for h in HALVES:
+            for i in range(W1_CUTS[k], W1_CUTS[k + 1]):
+                product(h, i, T.w1q, T.w1p, T.xq, T.xp, 0, "z")
+    for h in HALVES:
+        t.wait_ge(S["hq%d" % h], 1)
     t.wait_ge(S.q2, 1)
-    t.wait_ge(S.arr0, need[(core, "arr0")])
-    lo = NC - mine
-    for i in range(G):
-        t.matmul_mx(T.ps[:, 2048 + 512 * i:2048 + 512 * i + NC], T.w2q[:, W * i:W * i + W], T.w2p[:, W * i:W * i + W],
-                    T.cb[:, lo:lo + NC], T.cp[:, lo:lo + NC], True, True).then_inc(S["y%d" % i], 1)
-    t.wait_ge(S.gq, 1)
+    for h in HALVES:
+        if (core, "arr0%d" % h) in need:
+            t.wait_ge(S["arr0%d" % h], need[(core, "arr0%d" % h)])
+        for i in range(G):
+            product(h, i, T.w2q, T.w2p, T.cb, T.cp, NC - mine, "y")
+    for h in HALVES:
+        t.wait_ge(S["gq%d" % h], 1)
     t.wait_ge(S.q3, 1)
     t.wait_ge(S.arr1, need[(core, "arr1")])
     for i in range(2):
-        a = mine + W * i
-        t.matmul_mx(T.ps[:, 512 * i:512 * i + W], T.w3q[:], T.w3p[:], T.gb[:, a:a + W], T.gp[:, a:a + W],
-                    True, True).then_inc(S["f%d" % i], 1)
+        a = mine + H * i
+        t.matmul_mx(bank(0, i), T.w3q[:], T.w3p[:], T.gb[:, a:a + H], T.gp[:, a:a + H], True, True).then_inc(S["f%d" % i], 1)
 
-    sc = g.scalar
-    for base, tile, c, z, done in ((0, T.ht, C1, "z", S.ahs), (2048, T.gt, C2, "y", S.ags)):
-        for i in (0, 2):
-            sc.wait_ge(S[z + str(i)], 1)
-            sc.activation(tile[:, i:4 * NC:4], T.ps[:, base + 512 * i:base + 512 * i + NC], RELU,
-                          scale=c).then_inc(done, 1)
+    def act(tile, z, h, i, c, done):
+        out = tile[:, 4 * H * h + i:4 * H * h + 4 * H:4]
+        if i % 2 == 0:
+            sc.wait_ge(S["%s%d%d" % (z, h, i)], 1)
+            sc.activation(out, bank(h, i), RELU, scale=c).then_inc(S["%ss%d" % (done, h)], 1)
+        else:
+            v.wait_ge(S["%s%d%d" % (z, h, i)], 1)
+            v.tensor_scalar(out, bank(h, i), 0.0, c, AluOpType.max, AluOpType.mult).then_inc(S["%sv%d" % (done, h)], 1)
 
-    v = g.vector
-    v.wait_ge(S.xl, 32 if 0 < cut < NC else 16)
+    def pack(tile, q, p, lo, h, done):
+        v.wait_ge(S["%ss%d" % (done, h)], 2)
+        v.wait_ge(S["%sv%d" % (done, h)], 2)
+        v.quantize_mx(q[:, lo + H * h:lo + H * h + H], p[:, lo + H * h:lo + H * h + H],
+                      tile[:, 4 * H * h:4 * H * h + 4 * H]).then_inc(S["%sq%d" % (done, h)], 1)
+
+    v.wait_ge(S.xl, 16 * len(piece))
     v.quantize_mx(T.xq[:], T.xp[:], T.xs[:]).then_inc(S.qx, 1)
-    for k, (ld, q) in enumerate(((S.w1a, S.qa), (S.w1b, S.qb))):
-        v.wait_ge(ld, 16)
-        v.quantize_mx(T.w1q[:, 2 * W * k:2 * W * k + 2 * W], T.w1p[:, 2 * W * k:2 * W * k + 2 * W],
-                      T.w1s[:, half * k:half * k + half]).then_inc(q, 1)
-
-    def acts(base, tile, c, z, ds, dv):
-        for i in (1, 3):
-            v.wait_ge(S[z + str(i)], 1)
-            v.tensor_scalar(tile[:, i:4 * NC:4], T.ps[:, base + 512 * i:base + 512 * i + NC], 0.0, c,
-                            AluOpType.max, AluOpType.mult).then_inc(dv, 1)
-        v.wait_ge(ds, 2)
-        v.wait_ge(dv, 2)
-    acts(0, T.ht, C1, "z", S.ahs, S.ahv)
-    v.quantize_mx(T.cb[:, 0:NC], T.cp[:, 0:NC], T.ht[:]).then_inc(S.hq, 1)
+    for k in range(3):
+        a, b = W * W1_CUTS[k], W * W1_CUTS[k + 1]
+        v.wait_ge(S["w1l%d" % k], 16)
+        v.quantize_mx(T.w1q[:, a:b], T.w1p[:, a:b], T.w1s[:, 4 * a:4 * b]).then_inc(S["q1a%d" % k], 1)
+    for h, i in ((0, 0), (0, 1), (1, 0), (1, 1), (0, 2), (0, 3)):
+        act(T.ht, "z", h, i, C1, "h")
+    pack(T.ht, T.cb, T.cp, 0, 0, "h")
+    for h, i in ((1, 2), (1, 3)):
+        act(T.ht, "z", h, i, C1, "h")
+    pack(T.ht, T.cb, T.cp, 0, 1, "h")
     v.wait_ge(S.w2l, 16)
     v.quantize_mx(T.w2q[:], T.w2p[:], T.w2s[:]).then_inc(S.q2, 1)
     v.wait_ge(S.w3l, 16)
     v.quantize_mx(T.w3q[:], T.w3p[:], T.w3s[:]).then_inc(S.q3, 1)
-    acts(2048, T.gt, C2, "y", S.ags, S.agv)
-    v.quantize_mx(T.gb[:, NC:2 * NC], T.gp[:, NC:2 * NC], T.gt[:]).then_inc(S.gq, 1)
+    for h in HALVES:
+        for i in range(G):
+            act(T.gt, "y", h, i, C2, "g")
+        pack(T.gt, T.gb, T.gp, NC, h, "g")
 
     for i, done in ((0, S.yss), (1, S.ysv)):
-        pieces = [(a, b) for a, b in ((W * i, min(W * i + W, cut)), (max(W * i, cut), W * i + W)) if a < b]
         (sc if i == 0 else v).wait_ge(S["f%d" % i], 1)
-        for a, b in pieces:
-            k = (a - cut) % NC
-            src, out = T.ps[:, 512 * i + a - W * i:512 * i + b - W * i], T.ys[:, k:k + b - a]
+        k = 0
+        for p, o, w in piece:
+            a, b = max(p, H * i), min(p + w, H * i + H)
+            if a >= b:
+                continue
+            k += 1
+            src = T.ps[:, 512 * i + a - H * i:512 * i + b - H * i]
+            out = T.ys[:, o + a - p:o + b - p]
             if i == 0:
                 sc.activation(out, src, COPY).then_inc(done, 1)
             else:
                 v.tensor_copy(out, src).then_inc(done, 1)
-        g.sync.wait_ge(done, len(pieces))
+        g.sync.wait_ge(done, k)
     g.sync.dma_start(T.y[:], T.ys[:]).then_inc(S.st, 16)
     g.sync.wait_ge(S.st, 16)
 

@@ -7,6 +7,8 @@ H = 128
 W = 128
 G = 4
 C1, C2 = 0.023, 0.029
+EARLY = {3: (5, 6, 7, 10), 6: (2, 7, 9, 11), 9: (2, 5, 8, 10), 11: (7, 8, 9)}
+TURN = {(0, 2, 9): 0, (0, 6, 0): 5, (0, 6, 4): 1, (0, 7, 11): 1, (0, 10, 9): 1, (0, 11, 2): 1, (1, 3, 0): 5, (1, 7, 6): 1}
 
 CODES, BYTES = "float8_e4m3fn_x4", "uint8"
 SCRATCH = {
@@ -44,6 +46,10 @@ def may_chip(topo, src, cores, ch):
     return all(c == src or topo.may_write(src, c) for c in cores if topo.chip(c) == ch)
 
 
+def bound(topo, cores, j):
+    return [e for e in range(len(cores)) if not may_chip(topo, cores[j], cores, topo.chip(cores[e]))]
+
+
 def hit(items, target):
     best = {0: []}
     for name, size in items:
@@ -59,48 +65,54 @@ def orders(T, topo):
     ch = [topo.chip(c) for c in cores]
     oh, og = [], []
     for j in range(n):
+        far = bound(topo, cores, j)
+
+        def end(f):
+            return max([sum(cnt[j][e] for e in f[:k + 1]) for k, b in enumerate(f)
+                        if cnt[j][b] and j in bound(topo, cores, b)] or [0])
+        turns = [far[k:] + far[:k] for k in range(len(far)) if k == 0 or ch[far[k]] != ch[far[k - 1]]] or [[]]
+        far = min(turns, key=end)
         ring = [(j + 1 + k) % n for k in range(n)]
-        far = [e for e in sorted(ring) if not may_chip(topo, cores[j], cores, ch[e])]
         oh.append(far + [e for e in ring if e not in far])
     for e in range(n):
         src = [j for j in range(n) if j != e and cnt[j][e]]
-        late = [j for j in src if not may_chip(topo, cores[j], cores, ch[e])]
+        late = [j for j in src if e in bound(topo, cores, j)]
         near = [j for j in src if ch[j] == ch[e]]
         rest = [j for j in src if j not in late and j not in near]
         target = H - cnt[e][e]
-        early = None
-        if sum(cnt[j][e] for j in rest) >= target:
-            early = hit([(j, cnt[j][e]) for j in rest], target)
-        if early is None:
-            base = sum(cnt[j][e] for j in rest)
-            if base <= target:
-                more = hit([(j, cnt[j][e]) for j in near], target - base)
-                if more is not None:
-                    early = rest + more
+        base = sum(cnt[j][e] for j in rest)
+        early = hit([(j, cnt[j][e]) for j in rest], target)
+        if base <= target:
+            more = hit([(j, cnt[j][e]) for j in near], target - base)
+            if more is not None:
+                early = rest + more
         if early is None:
             early = hit([(j, cnt[j][e]) for j in rest + near], target)
         if early is None:
             early = rest
+        early = EARLY.get(e, early)
         tail = sorted([j for j in src if j not in early], key=lambda j: (j in near, j))
         og.append([e] + sorted(early) + tail + [j for j in range(n) if j != e and not cnt[j][e]])
     return oh, og
 
 
 def relays(cores, topo):
-    used, out = set(cores), {}
-    chips = sorted(set(topo.chip(c) for c in cores))
+    used, out = [], {}
     for j, s in enumerate(cores):
-        for ch in chips:
-            dst = [c for c in cores if topo.chip(c) == ch]
-            if may_chip(topo, s, cores, ch):
-                continue
-            pick = []
-            for near in (True, False):
-                r = [c for c in range(SIM_CORES) if c not in used and topo.mates(topo.chip(c), ch)
-                     and (topo.die(c) == topo.die(s)) == near
-                     and topo.may_write(s, c) and all(topo.may_write(c, d) for d in dst)][0]
-                used.add(r)
-                pick.append(r)
+        for ch in sorted(set(topo.chip(cores[e]) for e in bound(topo, cores, j))):
+            able = [c for c in range(SIM_CORES) if c not in cores and topo.may_write(s, c)
+                    and may_chip(topo, c, cores, ch)]
+            mate = [c for c in able if topo.mates(topo.chip(c), ch)]
+            home = [c for c in able if topo.chip(c) == topo.chip(s)]
+            pick = {}
+            for kind, pools in (("q", [mate]), ("p", [home, mate])):
+                free = [c for c in pools[0] if c not in used] or [c for c in pools[-1] if c not in used]
+
+                def busy(c):
+                    return (sum(topo.chip(u) == topo.chip(c) and topo.die(u) == topo.die(c) for u in used),
+                            topo.die(c) != topo.die(s), c)
+                pick[kind] = min(free, key=busy)
+                used.append(pick[kind])
             out[(j, ch)] = pick
     return out
 
@@ -129,6 +141,10 @@ def deal(items, src, load, topo):
     return res
 
 
+def width(t):
+    return t[6] * (4 if t[1] == "q" else 1)
+
+
 def plan(T, topo):
     cnt, cores = T.tables["CNT"], T.cores
     n = len(cores)
@@ -143,16 +159,15 @@ def plan(T, topo):
         return topo.chip(t[0]) != topo.chip(c)
 
     def fuse(c, wait, items):
-        groups = {}
-        for t in items:
-            groups.setdefault(t[6] * (4 if t[1] == "q" else 1), []).append(t)
-        cut = [(b, g[i:i + 8]) for b, g in groups.items() for i in range(0, len(g), 8)]
-
-        def rank(bg):
-            k = sum(far(c, t) for t in bg[1])
-            return (-min(k, 1), -k, -bg[0])
-        for b, g in sorted(cut, key=rank):
-            calls[c].append((wait, deal(g, c, load[c], topo)))
+        groups, cut = {}, []
+        for k, t in items:
+            groups.setdefault(width(t), []).append((k, t))
+        for b, g in groups.items():
+            g.sort(key=lambda x: x[0])
+            for part in (g[i:i + 8] for i in range(0, len(g), 8)):
+                cut.append((part[0][0], -sum(far(c, t) for k, t in part), -b, [t for k, t in part]))
+        for x in sorted(cut, key=lambda x: x[:3]):
+            calls[c].append((wait, deal(x[3], c, load[c], topo)))
 
     for ph in range(2):
         buf = {"q": ("cb", "gb")[ph], "p": ("cp", "gp")[ph]}
@@ -171,55 +186,51 @@ def plan(T, topo):
 
         def arr(a, b):
             return "arr0%d" % int(gpos[b][a] >= H) if ph == 0 else "arr1"
+        onward = []
         for a in range(n):
-            runs, direct, byrelay = {0: [], 1: []}, {0: [], 1: []}, set()
+            runs, direct, byrelay = {0: [], 1: []}, {0: [], 1: []}, bound(topo, cores, a)
             for (j, ch), pick in rel.items():
                 if j != a:
                     continue
-                dst = [b for b in range(n) if topo.chip(cores[b]) == ch]
-                byrelay.update(dst)
+                dst = [b for b in range(n) if topo.chip(cores[b]) == ch and cols(a, b)]
                 at = 0
                 for hf in HALVES:
-                    run = sorted((spot(a, b)[0], b) for b in dst if cols(a, b) and half(a, b) == hf)
                     part = []
-                    for p, b in run:
+                    for p, b in sorted((spot(a, b)[0], b) for b in dst if half(a, b) == hf):
                         if part and part[-1][0] + part[-1][1] == p:
                             part[-1][1] += cols(a, b)
                             part[-1][2].append(b)
                         else:
                             part.append([p, cols(a, b), [b]])
-                    for kind, r in zip("qp", pick):
-                        out, put = [], at
+                    for kind, r in pick.items():
+                        out, put, sem = [], at, "rel%d%d" % (ph, hf)
                         for p, w, bs in part:
-                            runs[hf].append((r, kind, buf[kind], p, rbuf[kind], put, w, "rel%d%d" % (ph, hf)))
-                            out += [(cores[b], kind, rbuf[kind], put + spot(a, b)[0] - p, buf[kind], spot(a, b)[1],
-                                     cols(a, b), arr(a, b)) for b in bs]
+                            runs[hf].append((0, (r, kind, buf[kind], p, rbuf[kind], put, w, sem)))
+                            out += [(0, (cores[b], kind, rbuf[kind], put + spot(a, b)[0] - p, buf[kind], spot(a, b)[1],
+                                         cols(a, b), arr(a, b))) for b in bs]
                             put += w
-                        fuse(r, "rel%d%d" % (ph, hf), out)
+                        onward.append((hf, r, sem, out))
                     at += sum(w for p, w, bs in part)
             for b in range(n):
                 if b == a or b in byrelay or not cols(a, b):
                     continue
                 for kind in "qp":
-                    direct[half(a, b)].append((cores[b], kind, buf[kind], spot(a, b)[0], buf[kind], spot(a, b)[1],
-                                               cols(a, b), arr(a, b)))
+                    t = (cores[b], kind, buf[kind], spot(a, b)[0], buf[kind], spot(a, b)[1], cols(a, b), arr(a, b))
+                    if ph == 0 and bound(topo, cores, b):
+                        k = 2
+                    elif not far(cores[a], t):
+                        k = 5
+                    else:
+                        k = 2 if ph == 1 else 3 if t[7] == "arr00" else 4
+                    direct[half(a, b)].append((TURN.get((ph, a, b), k), t))
             c, wait = cores[a], ["hq0", "hq1"] if ph == 0 else ["gq0", "gq1"]
-            if ph == 0:
-                soon = [t for t in direct[0] if far(c, t) and t[7] == "arr00"]
-                size = set(t[6] * (4 if t[1] == "q" else 1) for t in soon)
-                first = [t for t in direct[0] if t[6] * (4 if t[1] == "q" else 1) in size]
-                rest = [t for t in direct[0] if t not in first] + direct[1]
-                fuse(c, wait[0], runs[0])
-                fuse(c, wait[0], first)
-                fuse(c, wait[1], runs[1])
-                soon = [t for t in rest if far(c, t) and t[7] == "arr00"]
-                size = set(t[6] * (4 if t[1] == "q" else 1) for t in soon)
-                fuse(c, wait[1], [t for t in rest if t[6] * (4 if t[1] == "q" else 1) in size])
-                fuse(c, wait[1], [t for t in rest if t[6] * (4 if t[1] == "q" else 1) not in size])
-            else:
-                for hf in HALVES:
-                    fuse(c, wait[hf], runs[hf])
-                    fuse(c, wait[hf], direct[hf])
+            size = set(width(t) for k, t in direct[0] if k <= 2 or ph == 1)
+            fuse(c, wait[0], runs[0])
+            fuse(c, wait[0], [x for x in direct[0] if width(x[1]) in size])
+            fuse(c, wait[1], runs[1])
+            fuse(c, wait[1], [x for x in direct[0] if width(x[1]) not in size] + direct[1])
+        for hf, r, sem, out in sorted(onward, key=lambda x: x[0]):
+            fuse(r, sem, out)
     need, own = {}, {}
     for c in calls:
         for wait, group in calls[c]:
@@ -273,11 +284,12 @@ def rank_program(g, core, T, topo):
             piece.append([at, o, w])
         at += w
 
-    for k, (p, o, w) in enumerate(piece):
-        (g.sync if k % 2 == 0 else sc).dma_start(T.xs[:, 4 * p:4 * p + 4 * w], T.x[:, 4 * o:4 * o + 4 * w]).then_inc(S.xl, 16)
-    for k, q in enumerate((g.sync, sc, g.sync)):
+    loads = [(T.xs[:, 4 * p:4 * p + 4 * w], T.x[:, 4 * o:4 * o + 4 * w], S.xl) for p, o, w in piece]
+    for k in range(3):
         a, b = 4 * W * W1_CUTS[k], 4 * W * W1_CUTS[k + 1]
-        q.dma_start(T.w1s[:, a:b], T.w1[:, a:b]).then_inc(S["w1l%d" % k], 16)
+        loads.append((T.w1s[:, a:b], T.w1[:, a:b], S["w1l%d" % k]))
+    for k, (out, src, sem) in enumerate(loads):
+        (g.sync if k % 2 == 0 else sc).dma_start(out, src).then_inc(sem, 16)
     g.sync.dma_start(T.w2s[:], T.w2[:]).then_inc(S.w2l, 16)
     g.sync.dma_start(T.w3s[:], T.w3[:]).then_inc(S.w3l, 16)
 

from concourse.bass import DstId, RemoteDMATransfer
from concourse.mybir import dt, AluOpType, ActivationFunctionType

SIM_CORES = 64
NC = 256
H = 128
W = 128
G = 4
C1, C2 = 0.023, 0.029
EARLY = {3: (5, 6, 7, 10), 6: (2, 7, 9, 11), 9: (2, 5, 8, 10), 11: (7, 8, 9)}
TURN = {(0, 2, 9): 0, (0, 6, 0): 5, (0, 6, 4): 1, (0, 7, 11): 1, (0, 10, 9): 1, (0, 11, 2): 1, (1, 3, 0): 5, (1, 7, 6): 1}

CODES, BYTES = "float8_e4m3fn_x4", "uint8"
SCRATCH = {
    "xs": ("sbuf", [128, 4 * NC], "bfloat16"),
    "w1s": ("sbuf", [128, 4 * G * W], "bfloat16"),
    "w2s": ("sbuf", [128, 4 * G * W], "bfloat16"),
    "w3s": ("sbuf", [128, 4 * W], "bfloat16"),
    "ht": ("sbuf", [128, 4 * NC], "bfloat16"),
    "gt": ("sbuf", [128, 4 * NC], "bfloat16"),
    "ys": ("sbuf", [128, NC], "float32"),
    "xq": ("sbuf", [128, NC], CODES), "xp": ("sbuf", [128, NC], BYTES),
    "w1q": ("sbuf", [128, G * W], CODES), "w1p": ("sbuf", [128, G * W], BYTES),
    "w2q": ("sbuf", [128, G * W], CODES), "w2p": ("sbuf", [128, G * W], BYTES),
    "w3q": ("sbuf", [128, W], CODES), "w3p": ("sbuf", [128, W], BYTES),
    "cb": ("sbuf", [128, 2 * NC], CODES), "cp": ("sbuf", [128, 2 * NC], BYTES),
    "gb": ("sbuf", [128, 2 * NC], CODES), "gp": ("sbuf", [128, 2 * NC], BYTES),
    "rq0": ("sbuf", [128, NC], CODES), "rp0": ("sbuf", [128, NC], BYTES),
    "rq1": ("sbuf", [128, NC], CODES), "rp1": ("sbuf", [128, NC], BYTES),
    "ps": ("psum", [128, 4096], "float32"),
}
HALVES = (0, 1)
SEMAPHORES = (["xl", "w1l0", "w1l1", "w1l2", "w2l", "w3l", "qx", "q1a0", "q1a1", "q1a2", "q2", "q3", "f0", "f1",
               "ysv", "yss", "st", "loc", "arr00", "arr01", "arr1"]
              + ["rel%d%d" % (p, h) for p in HALVES for h in HALVES]
              + ["%s%d" % (s, h) for s in ("hq", "gq", "hs", "hv", "gs", "gv") for h in HALVES]
              + ["%s%d%d" % (s, h, i) for s in "zy" for h in HALVES for i in range(G)])
W1_CUTS = (0, 2, 3, 4)


def bits(m):
    return [k for k in range(16) if m >> k & 1]


def may_chip(topo, src, cores, ch):
    return all(c == src or topo.may_write(src, c) for c in cores if topo.chip(c) == ch)


def bound(topo, cores, j):
    return [e for e in range(len(cores)) if not may_chip(topo, cores[j], cores, topo.chip(cores[e]))]


def hit(items, target):
    best = {0: []}
    for name, size in items:
        for s in sorted(best, reverse=True):
            if s + size <= target and s + size not in best:
                best[s + size] = best[s] + [name]
    return best.get(target)


def orders(T, topo):
    cnt, cores = T.tables["CNT"], T.cores
    n = len(cores)
    ch = [topo.chip(c) for c in cores]
    oh, og = [], []
    for j in range(n):
        far = bound(topo, cores, j)

        def end(f):
            return max([sum(cnt[j][e] for e in f[:k + 1]) for k, b in enumerate(f)
                        if cnt[j][b] and j in bound(topo, cores, b)] or [0])
        turns = [far[k:] + far[:k] for k in range(len(far)) if k == 0 or ch[far[k]] != ch[far[k - 1]]] or [[]]
        far = min(turns, key=end)
        ring = [(j + 1 + k) % n for k in range(n)]
        oh.append(far + [e for e in ring if e not in far])
    for e in range(n):
        src = [j for j in range(n) if j != e and cnt[j][e]]
        late = [j for j in src if e in bound(topo, cores, j)]
        near = [j for j in src if ch[j] == ch[e]]
        rest = [j for j in src if j not in late and j not in near]
        target = H - cnt[e][e]
        base = sum(cnt[j][e] for j in rest)
        early = hit([(j, cnt[j][e]) for j in rest], target)
        if base <= target:
            more = hit([(j, cnt[j][e]) for j in near], target - base)
            if more is not None:
                early = rest + more
        if early is None:
            early = hit([(j, cnt[j][e]) for j in rest + near], target)
        if early is None:
            early = rest
        early = EARLY.get(e, early)
        tail = sorted([j for j in src if j not in early], key=lambda j: (j in near, j))
        og.append([e] + sorted(early) + tail + [j for j in range(n) if j != e and not cnt[j][e]])
    return oh, og


def relays(cores, topo):
    used, out = [], {}
    for j, s in enumerate(cores):
        for ch in sorted(set(topo.chip(cores[e]) for e in bound(topo, cores, j))):
            able = [c for c in range(SIM_CORES) if c not in cores and topo.may_write(s, c)
                    and may_chip(topo, c, cores, ch)]
            mate = [c for c in able if topo.mates(topo.chip(c), ch)]
            home = [c for c in able if topo.chip(c) == topo.chip(s)]
            pick = {}
            for kind, pools in (("q", [mate]), ("p", [home, mate])):
                free = [c for c in pools[0] if c not in used] or [c for c in pools[-1] if c not in used]

                def busy(c):
                    return (sum(topo.chip(u) == topo.chip(c) and topo.die(u) == topo.die(c) for u in used),
                            topo.die(c) != topo.die(s), c)
                pick[kind] = min(free, key=busy)
                used.append(pick[kind])
            out[(j, ch)] = pick
    return out


def deal(items, src, load, topo):
    away = [c for c in range(SIM_CORES) if topo.chip(c) != topo.chip(src)]
    off = bits(topo.mask(src, away[0]))
    res = []
    for far in (True, False):
        grp = [t for t in items if (topo.chip(t[0]) != topo.chip(src)) == far]
        if not grp:
            continue
        pool = off if far else [k for k in bits(topo.mask(src, grp[0][0])) if k not in off]
        size = [1] * len(grp)
        while True:
            k = min(range(len(grp)), key=lambda i: size[i])
            if sum(size) + size[k] > len(pool):
                break
            size[k] *= 2
        free = sorted(pool, key=lambda k: load[k])
        for i in sorted(range(len(grp)), key=lambda i: size[i]):
            eng, free = free[:size[i]], free[size[i]:]
            for k in eng:
                load[k] += 128 // size[i]
            res.append((grp[i], eng))
    return res


def width(t):
    return t[6] * (4 if t[1] == "q" else 1)


def plan(T, topo):
    cnt, cores = T.tables["CNT"], T.cores
    n = len(cores)
    oh, og = orders(T, topo)
    hpos = [{e: sum(cnt[j][f] for f in oh[j][:oh[j].index(e)]) for e in range(n)} for j in range(n)]
    gpos = [{j: sum(cnt[i][e] for i in og[e][:og[e].index(j)]) for j in range(n)} for e in range(n)]
    rel = relays(cores, topo)
    calls = {c: [] for c in range(SIM_CORES)}
    load = {c: [0] * 16 for c in range(SIM_CORES)}

    def far(c, t):
        return topo.chip(t[0]) != topo.chip(c)

    def fuse(c, wait, items):
        groups, cut = {}, []
        for k, t in items:
            groups.setdefault(width(t), []).append((k, t))
        for b, g in groups.items():
            g.sort(key=lambda x: x[0])
            for part in (g[i:i + 8] for i in range(0, len(g), 8)):
                cut.append((part[0][0], -sum(far(c, t) for k, t in part), -b, [t for k, t in part]))
        for x in sorted(cut, key=lambda x: x[:3]):
            calls[c].append((wait, deal(x[3], c, load[c], topo)))

    for ph in range(2):
        buf = {"q": ("cb", "gb")[ph], "p": ("cp", "gp")[ph]}
        rbuf = {"q": "rq%d" % ph, "p": "rp%d" % ph}

        def cols(a, b):
            return cnt[a][b] if ph == 0 else cnt[b][a]

        def spot(a, b):
            if ph == 0:
                return hpos[a][b], NC + gpos[b][a] - cnt[b][b]
            return NC + gpos[a][b], cnt[b][b] + hpos[b][a]

        def half(a, b):
            return int(spot(a, b)[0] % NC + cols(a, b) > H)

        def arr(a, b):
            return "arr0%d" % int(gpos[b][a] >= H) if ph == 0 else "arr1"
        onward = []
        for a in range(n):
            runs, direct, byrelay = {0: [], 1: []}, {0: [], 1: []}, bound(topo, cores, a)
            for (j, ch), pick in rel.items():
                if j != a:
                    continue
                dst = [b for b in range(n) if topo.chip(cores[b]) == ch and cols(a, b)]
                at = 0
                for hf in HALVES:
                    part = []
                    for p, b in sorted((spot(a, b)[0], b) for b in dst if half(a, b) == hf):
                        if part and part[-1][0] + part[-1][1] == p:
                            part[-1][1] += cols(a, b)
                            part[-1][2].append(b)
                        else:
                            part.append([p, cols(a, b), [b]])
                    for kind, r in pick.items():
                        out, put, sem = [], at, "rel%d%d" % (ph, hf)
                        for p, w, bs in part:
                            runs[hf].append((0, (r, kind, buf[kind], p, rbuf[kind], put, w, sem)))
                            out += [(0, (cores[b], kind, rbuf[kind], put + spot(a, b)[0] - p, buf[kind], spot(a, b)[1],
                                         cols(a, b), arr(a, b))) for b in bs]
                            put += w
                        onward.append((hf, r, sem, out))
                    at += sum(w for p, w, bs in part)
            for b in range(n):
                if b == a or b in byrelay or not cols(a, b):
                    continue
                for kind in "qp":
                    t = (cores[b], kind, buf[kind], spot(a, b)[0], buf[kind], spot(a, b)[1], cols(a, b), arr(a, b))
                    if ph == 0 and bound(topo, cores, b):
                        k = 2
                    elif not far(cores[a], t):
                        k = 5
                    else:
                        k = 2 if ph == 1 else 3 if t[7] == "arr00" else 4
                    direct[half(a, b)].append((TURN.get((ph, a, b), k), t))
            c, wait = cores[a], ["hq0", "hq1"] if ph == 0 else ["gq0", "gq1"]
            size = set(width(t) for k, t in direct[0] if k <= 2 or ph == 1)
            fuse(c, wait[0], runs[0])
            fuse(c, wait[0], [x for x in direct[0] if width(x[1]) in size])
            fuse(c, wait[1], runs[1])
            fuse(c, wait[1], [x for x in direct[0] if width(x[1]) not in size] + direct[1])
        for hf, r, sem, out in sorted(onward, key=lambda x: x[0]):
            fuse(r, sem, out)
    need, own = {}, {}
    for c in calls:
        for wait, group in calls[c]:
            for t, eng in group:
                need[(t[0], t[7])] = need.get((t[0], t[7]), 0) + len(eng)
                own[c] = own.get(c, 0) + len(eng)
    return calls, need, own


def remote(g, core, T, topo, calls, need, own):
    waited = set()
    for wait, group in calls[core]:
        if wait not in waited:
            waited.add(wait)
            g.wait_ge(T.sem[wait], need.get((core, wait), 1))
        tr = []
        for (dst, kind, sb, sc, db, dc, w, sem), eng in group:
            src, out = T[sb][:, sc:sc + w], T[db][:, dc:dc + w]
            if kind == "q":
                src, out = src.bitcast(dt.uint8), out.bitcast(dt.uint8)
            rid, pid, _ = topo.addr(dst)
            tr.append((rid, pid, src, out, sum(1 << k for k in eng), T.sem[sem]))
        if len(tr) == 1:
            rid, pid, src, out, m, s = tr[0]
            g.remote_dma(out, src, s, T.sem.loc, pid, rid, m)
        else:
            g.remote_dma_fused([RemoteDMATransfer(dst_ids=[DstId(rid=rid, pnc=pid)], dma_engine_mask=m, remote_sem=s,
                                                  src=src, dst=out) for rid, pid, src, out, m, s in tr],
                               local_sem=T.sem.loc)
    if core in own:
        g.wait_ge(T.sem.loc, own[core])


def rank_program(g, core, T, topo):
    calls, need, own = plan(T, topo)
    rank = T.rank_of(core)
    if rank is None:
        remote(g, core, T, topo, calls, need, own)
        return
    cnt, S = T.tables["CNT"], T.sem
    mine = cnt[rank][rank]
    RELU, COPY = ActivationFunctionType.Relu, ActivationFunctionType.Copy
    t, sc, v = g.tensor, g.scalar, g.vector

    piece, at = [], 0
    for e in orders(T, topo)[0][rank]:
        o, w = sum(cnt[rank][:e]), cnt[rank][e]
        if w and piece and piece[-1][1] + piece[-1][2] == o:
            piece[-1][2] += w
        elif w:
            piece.append([at, o, w])
        at += w

    loads = [(T.xs[:, 4 * p:4 * p + 4 * w], T.x[:, 4 * o:4 * o + 4 * w], S.xl) for p, o, w in piece]
    for k in range(3):
        a, b = 4 * W * W1_CUTS[k], 4 * W * W1_CUTS[k + 1]
        loads.append((T.w1s[:, a:b], T.w1[:, a:b], S["w1l%d" % k]))
    for k, (out, src, sem) in enumerate(loads):
        (g.sync if k % 2 == 0 else sc).dma_start(out, src).then_inc(sem, 16)
    g.sync.dma_start(T.w2s[:], T.w2[:]).then_inc(S.w2l, 16)
    g.sync.dma_start(T.w3s[:], T.w3[:]).then_inc(S.w3l, 16)

    def bank(h, i):
        return T.ps[:, 2048 * h + 512 * i:2048 * h + 512 * i + H]

    def product(h, i, w, wp, m, mp, lo, sem):
        t.matmul_mx(bank(h, i), w[:, W * i:W * i + W], wp[:, W * i:W * i + W], m[:, lo + H * h:lo + H * h + H],
                    mp[:, lo + H * h:lo + H * h + H], True, True).then_inc(S["%s%d%d" % (sem, h, i)], 1)
    t.wait_ge(S.qx, 1)
    for k in range(3):
        t.wait_ge(S["q1a%d" % k], 1)
        for h in HALVES:
            for i in range(W1_CUTS[k], W1_CUTS[k + 1]):
                product(h, i, T.w1q, T.w1p, T.xq, T.xp, 0, "z")
    for h in HALVES:
        t.wait_ge(S["hq%d" % h], 1)
    t.wait_ge(S.q2, 1)
    for h in HALVES:
        if (core, "arr0%d" % h) in need:
            t.wait_ge(S["arr0%d" % h], need[(core, "arr0%d" % h)])
        for i in range(G):
            product(h, i, T.w2q, T.w2p, T.cb, T.cp, NC - mine, "y")
    for h in HALVES:
        t.wait_ge(S["gq%d" % h], 1)
    t.wait_ge(S.q3, 1)
    t.wait_ge(S.arr1, need[(core, "arr1")])
    for i in range(2):
        a = mine + H * i
        t.matmul_mx(bank(0, i), T.w3q[:], T.w3p[:], T.gb[:, a:a + H], T.gp[:, a:a + H], True, True).then_inc(S["f%d" % i], 1)

    def act(tile, z, h, i, c, done):
        out = tile[:, 4 * H * h + i:4 * H * h + 4 * H:4]
        if i % 2 == 0:
            sc.wait_ge(S["%s%d%d" % (z, h, i)], 1)
            sc.activation(out, bank(h, i), RELU, scale=c).then_inc(S["%ss%d" % (done, h)], 1)
        else:
            v.wait_ge(S["%s%d%d" % (z, h, i)], 1)
            v.tensor_scalar(out, bank(h, i), 0.0, c, AluOpType.max, AluOpType.mult).then_inc(S["%sv%d" % (done, h)], 1)

    def pack(tile, q, p, lo, h, done):
        v.wait_ge(S["%ss%d" % (done, h)], 2)
        v.wait_ge(S["%sv%d" % (done, h)], 2)
        v.quantize_mx(q[:, lo + H * h:lo + H * h + H], p[:, lo + H * h:lo + H * h + H],
                      tile[:, 4 * H * h:4 * H * h + 4 * H]).then_inc(S["%sq%d" % (done, h)], 1)

    v.wait_ge(S.xl, 16 * len(piece))
    v.quantize_mx(T.xq[:], T.xp[:], T.xs[:]).then_inc(S.qx, 1)
    for k in range(3):
        a, b = W * W1_CUTS[k], W * W1_CUTS[k + 1]
        v.wait_ge(S["w1l%d" % k], 16)
        v.quantize_mx(T.w1q[:, a:b], T.w1p[:, a:b], T.w1s[:, 4 * a:4 * b]).then_inc(S["q1a%d" % k], 1)
    for h, i in ((0, 0), (0, 1), (1, 0), (1, 1), (0, 2), (0, 3)):
        act(T.ht, "z", h, i, C1, "h")
    pack(T.ht, T.cb, T.cp, 0, 0, "h")
    for h, i in ((1, 2), (1, 3)):
        act(T.ht, "z", h, i, C1, "h")
    pack(T.ht, T.cb, T.cp, 0, 1, "h")
    v.wait_ge(S.w2l, 16)
    v.quantize_mx(T.w2q[:], T.w2p[:], T.w2s[:]).then_inc(S.q2, 1)
    v.wait_ge(S.w3l, 16)
    v.quantize_mx(T.w3q[:], T.w3p[:], T.w3s[:]).then_inc(S.q3, 1)
    for h in HALVES:
        for i in range(G):
            act(T.gt, "y", h, i, C2, "g")
        pack(T.gt, T.gb, T.gp, NC, h, "g")

    for i, done in ((0, S.yss), (1, S.ysv)):
        (sc if i == 0 else v).wait_ge(S["f%d" % i], 1)
        k = 0
        for p, o, w in piece:
            a, b = max(p, H * i), min(p + w, H * i + H)
            if a >= b:
                continue
            k += 1
            src = T.ps[:, 512 * i + a - H * i:512 * i + b - H * i]
            out = T.ys[:, o + a - p:o + b - p]
            if i == 0:
                sc.activation(out, src, COPY).then_inc(done, 1)
            else:
                v.tensor_copy(out, src).then_inc(done, 1)
        g.sync.wait_ge(done, k)
    g.sync.dma_start(T.y[:], T.ys[:]).then_inc(S.st, 16)
    g.sync.wait_ge(S.st, 16)

    remote(g, core, T, topo, calls, need, own)
